import numpy as np
import ml_dtypes


def mxq(x, axis, fmt="e4m3"):
    dtype, down = {"e4m3": (ml_dtypes.float8_e4m3fn, 7), "e5m2": (ml_dtypes.float8_e5m2, 14)}[fmt]
    v = np.moveaxis(np.asarray(x, np.float32).astype(ml_dtypes.bfloat16).astype(np.float64), axis, -1)
    blocks = v.reshape(v.shape[:-1] + (-1, 32))
    amax = np.abs(blocks).max(-1, keepdims=True)
    byte = np.maximum(np.where(amax > 0, np.frexp(amax)[1] - 1 + 127, 0) - down, 1)
    scale = np.exp2(byte - 127.0)
    codes = (blocks / scale).astype(np.float32).astype(dtype).astype(np.float64)
    return np.moveaxis((codes * scale).reshape(v.shape), -1, axis)


WIDE = False


def mx_kscale(k):
    if not WIDE:
        return np.ones(k)
    levels = np.array([10, -10, 5, -5, 0])
    if k % 512:
        return np.exp2(np.random.permutation(np.resize(levels, k // 32))).repeat(32)
    a = np.empty((k // 512, 16))
    for p in range(k // 512):
        a[p, :8] = np.random.permutation(np.resize(levels, 8))
        for g in range(8):
            far = levels[np.abs(levels - a[p, g]) >= 10]
            a[p, g + 8] = far[np.random.randint(len(far))]
    return np.exp2(a.ravel()).repeat(32)


def f64(x):
    return np.asarray(x).astype(np.float64)


def striped(idx):
    return np.tile(idx.reshape(-1, 16).T, (8, 1)).astype(np.uint16)


def unstriped(offs):
    return offs[:16].T.reshape(-1).astype(np.int64)


def striped8(idx):
    return np.concatenate([x.reshape(-1, 16).T for x in idx]).astype(np.uint16)


def runs(offs, k):
    lists = np.stack([offs[16 * r : 16 * r + 16].T.reshape(-1) for r in range(8)]).astype(np.int64)
    return lists[np.arange(k) % 512 // 64]


def pack_weight(w):
    k, n = w.shape
    w = f64(np.asarray(w, np.float32).astype(ml_dtypes.bfloat16)).reshape(k // 32, 32, n)
    amax = np.abs(w).max(1)
    byte = np.clip(np.where(amax > 0, np.frexp(amax)[1] - 1 + 127 - 7, 1), 1, 254)
    scaled = (w * np.exp2(127.0 - byte)[:, None, :]).reshape(k, n).astype(np.float32)
    words = np.ascontiguousarray(scaled.reshape(k // 512, 128, 4, n).transpose(0, 1, 3, 2)).astype(ml_dtypes.float8_e4m3fn).view(np.uint8)
    return words, np.ascontiguousarray(byte.astype(np.uint8).reshape(k // 512, 16, n))


def unpack_weight(words, scales):
    g, p, n, _ = words.shape
    vals = np.ascontiguousarray(words).view(ml_dtypes.float8_e4m3fn).astype(np.float64) * np.repeat(np.exp2(scales.astype(np.float64) - 127.0), 8, axis=1)[..., None]
    return vals.transpose(0, 1, 3, 2).reshape(g * 512, n)


def sigmoid(v):
    return 1.0 / (1.0 + np.exp(-np.maximum(v, -700.0)))


K, T, S, V, H = 512, 2048, 512, 512, 512


def setup_inputs():
    n = np.random.standard_normal
    s = mx_kscale(K)[:, None]
    u = mx_kscale(S)
    packed_xT = pack_weight(n((K, T)) * s)
    return {
        "x_words": packed_xT[0],
        "x_scales": packed_xT[1],
        "w1": (n((K, H)) / np.sqrt(K) / s).astype(np.float32),
        "w2": (n((K, H)) / np.sqrt(K) / s).astype(np.float32),
        "ga": (np.random.uniform(0.5, 1.5, (H, 1)) * u[:, None]).astype(np.float32),
        "gb": (np.random.uniform(0.5, 1.5, (H, 1)) / u[:, None]).astype(np.float32),
        "offs": striped(np.random.permutation(T)[:S]),
        "two": striped(np.random.permutation(T)[:V]),
        "n1": striped8(np.stack([np.random.permutation(S) for _ in range(8)])),
        "n2": striped8(np.stack([np.random.permutation(S) for _ in range(8)])),
        "n3": striped8(np.stack([np.random.permutation(S) for _ in range(8)])),
        "n4": striped8(np.stack([np.random.permutation(S) for _ in range(8)])),
        "n5": striped8(np.stack([np.random.permutation(V) for _ in range(8)])),
        "n6": striped8(np.stack([np.random.permutation(V) for _ in range(8)])),
        "n7": striped8(np.stack([np.random.permutation(V) for _ in range(8)])),
        "n8": striped8(np.stack([np.random.permutation(V) for _ in range(8)])),
        "n9": striped8(np.stack([np.random.permutation(V) for _ in range(8)])),
        "n10": striped8(np.stack([np.random.permutation(V) for _ in range(8)])),
    }


def reference(x_words, x_scales, w1, w2, ga, gb, offs, two, n1, n2, n3, n4, n5, n6, n7, n8, n9, n10):
    xq = unpack_weight(x_words, x_scales)[:, unstriped(offs)]
    a = mxq(f64(w1), 0, "e4m3").T @ xq
    z = f64(ga) * (0.75 * ((a[np.arange(H)[:, None], runs(n1, H)]) * (a[np.arange(H)[:, None], runs(n2, H)]) - ((a[np.arange(H)[:, None], runs(n3, H)]) * (a[np.arange(H)[:, None], runs(n4, H)]))))
    x_two = unpack_weight(x_words, x_scales)[:, unstriped(two)]
    b = mxq(f64(w2), 0, "e4m3").T @ x_two
    z2 = f64(gb) * ((b[np.arange(H)[:, None], runs(n5, H)]) * sigmoid(b) + (b[np.arange(H)[:, None], runs(n6, H)]) * (sigmoid(b[np.arange(H)[:, None], runs(n7, H)])))
    s = 0.0625 * ((mxq(z, 0, "e4m3").T @ mxq(z2, 0, "e4m3")))
    b1 = s[np.arange(S)[:, None], runs(n8, S)]
    b2 = s[np.arange(S)[:, None], runs(n9, S)]
    b3 = s[np.arange(S)[:, None], runs(n10, S)]
    return np.maximum(np.maximum(b1, b2), b3) - (0.5 * (np.maximum(np.minimum(b1, b2), np.minimum(np.maximum(b1, b2), b3))))

@@ -1,0 +1,196 @@
+from contextlib import ExitStack
+
+import concourse.mybir as mybir
+
+F32 = mybir.dt.float32
+BF16 = mybir.dt.bfloat16
+I32 = mybir.dt.int32
+U32 = mybir.dt.uint32
+U16 = mybir.dt.uint16
+U8 = mybir.dt.uint8
+FP8X4 = mybir.dt.float8_e4m3fn_x4
+ALU = mybir.AluOpType
+ACT = mybir.ActivationFunctionType
+
+P = 128
+PACK = 4
+T = 2048
+N = 512
+WINDOW = 2 * N
+HALF = N // 2
+FLOPS = 3 * 2 * 512 * 512 * 512
+
+
+def tile_picked_kqdetwsumtop2_none_p_kernel(
+    tc, x_words, x_scales, w1, w2, ga, gb, offs, two, n1, n2, n3, n4, n5, n6, n7, n8, n9, n10, out
+):
+    nc = tc.nc
+    with ExitStack() as ctx:
+        keep = ctx.enter_context(tc.tile_pool(name="keep", bufs=1))
+        work = ctx.enter_context(tc.tile_pool(name="work", bufs=2))
+        psum = ctx.enter_context(tc.psum_pool(name="psum", bufs=1))
+
+        def load_list(name, source):
+            tile = keep.tile([P, N // 16], U16, name=name)
+            nc.sync.dma_start(tile[:], source)
+            return tile
+
+        def load_weight(name, w):
+            halves = []
+            for h in range(2):
+                raw = keep.tile([P, PACK, HALF], F32, name=f"{name}_raw{h}")
+                nc.sync.dma_start(raw[:], w.rearrange("(p j) c -> p j c", j=PACK)[:, :, h * HALF : (h + 1) * HALF])
+                halves.append(raw)
+            return halves
+
+        def load_gain(name, gain, queue):
+            tile = keep.tile([P, 8], F32, name=name)
+            rows = gain.rearrange("(a e) o -> a (e o)", e=8)
+            for i in range(2):
+                queue.dma_start(tile[i:P:2, 0:7], rows[:, i : i + 7])
+            return tile
+
+        def cast_weight(name, halves):
+            grouped = keep.tile([P, N * PACK], BF16, name=f"{name}_bf", align_bytes=64)
+            dealt = grouped[:].rearrange("p (t a i j) -> p t a j i", t=4, i=2, j=PACK)
+            for h, raw in enumerate(halves):
+                nc.scalar.copy(dealt[:, :, 32 * h : 32 * (h + 1)], raw[:].rearrange("p j (a t i) -> p t a j i", t=4, i=2))
+            return grouped
+
+        def quantize(name, values, width):
+            codes = keep.tile([P, width], U32, name=f"{name}_codes", align_bytes=64)
+            scales = keep.tile([P, width], U8, name=f"{name}_scales", align_bytes=64)
+            nc.vector.quantize_mx(out=codes[:].bitcast(FP8X4), scales=scales[:], in_=values)
+            return codes, scales
+
+        def product(acc, lhs, lhs_cols, rhs):
+            nc.tensor.matmul_mx(
+                out=acc,
+                lhsT=lhs[0][:, lhs_cols].bitcast(FP8X4),
+                lhsT_scale=lhs[1][:, lhs_cols],
+                rhs=rhs[0][:].bitcast(FP8X4),
+                rhs_scale=rhs[1][:],
+                start=True,
+                stop=True,
+            )
+
+        scale_table = keep.tile([P, T], U8, name="scale_table")
+        nc.vector.memset(scale_table[:].bitcast(I32), 0)
+        windows = [keep.tile([P, WINDOW], F32, name=f"window{u}") for u in range(9)]
+        for window in windows:
+            nc.vector.memset(window[:, N:], 0.0)
+        plain_win, gained_win, raw_b = windows[0:4], windows[4:8], windows[8]
+        warm = keep.tile([P, 1], F32, name="warm")
+        nc.scalar.activation(warm[:], raw_b[:, N : N + 1], ACT.Sigmoid)
+
+        l_offs, l_two, l1, l3 = (load_list(f"l_{k}", n) for k, n in (("offs", offs), ("two", two), (1, n1), (3, n3)))
+        w1_raw = load_weight("w1", w1)
+        word_table = keep.tile([P, T], U32, name="word_table")
+        nc.sync.dma_start(word_table[:].bitcast(I32), x_words[0].rearrange("p n t -> p (n t)").bitcast(I32))
+        for q in range(4):
+            nc.sync.dma_start(scale_table[32 * q : 32 * q + 4, :].bitcast(I32), x_scales[0, 4 * q : 4 * q + 4, :].bitcast(I32))
+        ga_t = load_gain("ga_t", ga, nc.gpsimd)
+        l2, l4 = (load_list(f"l_{k}", n) for k, n in ((2, n2), (4, n4)))
+        w2_raw = load_weight("w2", w2)
+        gb_t = load_gain("gb_t", gb, nc.sync)
+        l7, l5, l6, l9, l8, l10 = (load_list(f"l{k}", n) for k, n in ((7, n7), (5, n5), (6, n6), (9, n9), (8, n8), (10, n10)))
+
+        picked = []
+        for name in ("xa", "xb"):
+            codes = keep.tile([P, N], U32, name=f"{name}_codes", align_bytes=64)
+            scales = keep.tile([P, N], U8, name=f"{name}_scales", align_bytes=64)
+            picked.append((codes, scales))
+        xa, xb = picked
+        nc.vector.tensor_copy(xa[1][:], scale_table[:].indirect(l_offs[:]))
+        w1q = quantize("w1", cast_weight("w1", w1_raw)[:], N)
+        nc.vector.tensor_copy(xa[0][:], word_table[:].indirect(l_offs[:]))
+        nc.vector.tensor_copy(xb[1][:], scale_table[:].indirect(l_two[:]))
+        nc.vector.tensor_copy(xb[0][:], word_table[:].indirect(l_two[:]))
+
+        banks = [psum.tile([P, N], F32, name=f"bank{u}") for u in range(8)]
+        for t in range(4):
+            product(banks[t][:], w1q, slice(P * t, P * (t + 1)), xa)
+            nc.scalar.activation(gained_win[t][:, :N], banks[t][:], ACT.Copy, scale=ga_t[:, 2 * t : 2 * t + 1])
+            nc.scalar.activation(plain_win[t][:, :N], banks[t][:], ACT.Copy, scale=0.75)
+
+        w2q = quantize("w2", cast_weight("w2", w2_raw)[:], N)
+        sig_own = keep.tile([P, PACK, N], F32, name="sig_own")
+        sig_other = keep.tile([P, PACK, N], F32, name="sig_other")
+        for t in range(4):
+            product(banks[4 + t][:], w2q, slice(P * t, P * (t + 1)), xb)
+            nc.scalar.activation(sig_own[:, t, :], banks[4 + t][:], ACT.Sigmoid)
+            nc.scalar.copy(raw_b[:, :N], banks[4 + t][:])
+            nc.scalar.activation(sig_other[:, t, :], raw_b[:].indirect(l7[:]), ACT.Sigmoid)
+
+        p12 = keep.tile([P, PACK, N], F32, name="p12")
+        p34 = keep.tile([P, PACK, N], F32, name="p34")
+        for t in range(4):
+            a1 = work.tile([P, N], F32, name="a1")
+            a3 = work.tile([P, N], F32, name="a3")
+            nc.vector.tensor_copy(a1[:], gained_win[t][:].indirect(l1[:]))
+            nc.vector.tensor_copy(a3[:], gained_win[t][:].indirect(l3[:]))
+            nc.vector.tensor_tensor(p12[:, t, :], plain_win[t][:].indirect(l2[:]), a1[:], ALU.mult)
+            nc.vector.tensor_tensor(p34[:, t, :], plain_win[t][:].indirect(l4[:]), a3[:], ALU.mult)
+            nc.scalar.activation(plain_win[t][:, :N], banks[4 + t][:], ACT.Copy, scale=gb_t[:, 2 * t : 2 * t + 1])
+
+        def make_z(t):
+            z_bf = keep.tile([P, P * PACK], BF16, name=f"z_bf{t}", align_bytes=64)
+            nc.vector.tensor_tensor(
+                z_bf[:].rearrange("p (a i k) -> p a k i", i=2, k=PACK),
+                p12[:].rearrange("p k (a t i) -> p t a k i", t=4, i=2)[:, t],
+                p34[:].rearrange("p k (a t i) -> p t a k i", t=4, i=2)[:, t],
+                ALU.subtract,
+            )
+            return z_bf
+
+        p5 = keep.tile([P, PACK, N], F32, name="p5")
+        p6 = keep.tile([P, PACK, N], F32, name="p6")
+        z_bf = [make_z(0)]
+        for t in range(4):
+            nc.vector.tensor_tensor(p5[:, t, :], plain_win[t][:].indirect(l5[:]), sig_own[:, t, :], ALU.mult)
+            nc.vector.tensor_tensor(p6[:, t, :], plain_win[t][:].indirect(l6[:]), sig_other[:, t, :], ALU.mult)
+        zq = [quantize("z0", z_bf[0][:], P)]
+
+        z2_bf = []
+        for h in range(2):
+            half_bf = keep.tile([P, HALF * PACK], BF16, name=f"z2_bf{h}", align_bytes=64)
+            cols = slice(h * HALF, (h + 1) * HALF)
+            nc.vector.tensor_tensor(
+                half_bf[:].rearrange("p (a i k) -> p a k i", i=2, k=PACK),
+                p5[:, :, cols].rearrange("p k (a i) -> p a k i", i=2),
+                p6[:, :, cols].rearrange("p k (a i) -> p a k i", i=2),
+                ALU.add,
+            )
+            z2_bf.append(half_bf)
+        z2q = [quantize(f"z2_{h}", z2_bf[h][:], HALF) for h in range(2)]
+        z_bf.extend(make_z(t) for t in range(1, 4))
+        zq.extend(quantize(f"z{t}", z_bf[t][:], P) for t in range(1, 4))
+
+        for t in range(4):
+            for h in range(2):
+                cols = slice(h * HALF, (h + 1) * HALF)
+                product(banks[t][:, cols], zq[t], slice(0, P), z2q[h])
+            nc.scalar.activation(gained_win[t][:, :N], banks[t][:], ACT.Copy, scale=0.03125)
+
+        out_rows = out.rearrange("(a t i) v -> t i a v", t=4, i=2)
+        for pair in ((0, 1), (2, 3)):
+            names = ("b2", "d12", "gap", "hi", "d3", "y", "bend", "res")
+            v = {(name, t): work.tile([P, N], F32, name=name) for name in names for t in pair}
+            for t in pair:
+                nc.vector.tensor_copy(v["b2", t][:], gained_win[t][:].indirect(l9[:]))
+            for t in pair:
+                nc.vector.tensor_tensor(v["d12", t][:], gained_win[t][:].indirect(l8[:]), v["b2", t][:], ALU.subtract)
+                nc.scalar.activation(v["gap", t][:], v["d12", t][:], ACT.Abs)
+            for t in pair:
+                nc.vector.scalar_tensor_tensor(v["hi", t][:], v["d12", t][:], 0.0, v["b2", t][:], ALU.max, ALU.add)
+            for t in pair:
+                nc.vector.tensor_tensor(v["d3", t][:], gained_win[t][:].indirect(l10[:]), v["hi", t][:], ALU.subtract)
+            for t in pair:
+                nc.vector.scalar_tensor_tensor(v["y", t][:], v["gap", t][:], -1.0, v["d3", t][:], ALU.mult, ALU.max)
+            for t in pair:
+                nc.vector.scalar_tensor_tensor(v["bend", t][:], v["y", t][:], -2.0, v["y", t][:], ALU.mult, ALU.min)
+            for t in pair:
+                for cols in (slice(0, HALF), slice(HALF, N)) if t == 3 else (slice(0, N),):
+                    nc.vector.tensor_tensor(v["res", t][:, cols], v["hi", t][:, cols], v["bend", t][:, cols], ALU.subtract)
+                    for i in range(2):
+                        nc.sync.dma_start(out_rows[t, i][:, cols], v["res", t][i:P:2, cols])

@@ -1,6 +1,7 @@
 from contextlib import ExitStack
 
 import concourse.mybir as mybir
+from concourse.masks import make_identity
 
 F32 = mybir.dt.float32
 BF16 = mybir.dt.bfloat16
@@ -35,13 +36,10 @@ def tile_picked_kqdetwsumtop2_none_p_kernel(
             nc.sync.dma_start(tile[:], source)
             return tile
 
-        def load_weight(name, w):
-            halves = []
-            for h in range(2):
-                raw = keep.tile([P, PACK, HALF], F32, name=f"{name}_raw{h}")
-                nc.sync.dma_start(raw[:], w.rearrange("(p j) c -> p j c", j=PACK)[:, :, h * HALF : (h + 1) * HALF])
-                halves.append(raw)
-            return halves
+        def load_half(name, w, h):
+            raw = keep.tile([P, PACK, HALF], F32, name=f"{name}_raw{h}")
+            nc.sync.dma_start(raw[:], w.rearrange("(p j) c -> p j c", j=PACK)[:, :, h * HALF : (h + 1) * HALF])
+            return raw
 
         def load_gain(name, gain, queue):
             tile = keep.tile([P, 8], F32, name=name)
@@ -74,24 +72,34 @@ def tile_picked_kqdetwsumtop2_none_p_kernel(
                 stop=True,
             )
 
+        def turn(bank, region, terms):
+            for u, term in enumerate(terms):
+                nc.tensor.matmul(
+                    bank[:, P * region : P * (region + 1)], term, ident[:], is_transpose=True, start=(u == 0), stop=(u == len(terms) - 1)
+                )
+
         scale_table = keep.tile([P, T], U8, name="scale_table")
         nc.vector.memset(scale_table[:].bitcast(I32), 0)
-        windows = [keep.tile([P, WINDOW], F32, name=f"window{u}") for u in range(9)]
-        for window in windows:
-            nc.vector.memset(window[:, N:], 0.0)
-        plain_win, gained_win, raw_b = windows[0:4], windows[4:8], windows[8]
-        warm = keep.tile([P, 1], F32, name="warm")
-        nc.scalar.activation(warm[:], raw_b[:, N : N + 1], ACT.Sigmoid)
+        windows = [keep.tile([P, WINDOW], F32, name=f"window{u}") for u in range(13)]
+        gained_win, plain_win, b_win, raw_b = windows[0:4], windows[4:8], windows[8:12], windows[12]
+        for window in windows[0:5]:
+            nc.vector.memset(window[:, N:].bitcast(I32), 0)
+        for window in windows[5:8]:
+            nc.scalar.activation(window[:, N:], windows[0][:, N:], ACT.Sigmoid)
 
-        l_offs, l_two, l1, l3 = (load_list(f"l_{k}", n) for k, n in (("offs", offs), ("two", two), (1, n1), (3, n3)))
-        w1_raw = load_weight("w1", w1)
-        word_table = keep.tile([P, T], U32, name="word_table")
-        nc.sync.dma_start(word_table[:].bitcast(I32), x_words[0].rearrange("p n t -> p (n t)").bitcast(I32))
+        ident = keep.tile([P, P], F32, name="ident")
+        make_identity(nc, ident[:])
+
+        l_offs, l_two = load_list("l_offs", offs), load_list("l_two", two)
+        w1_raw = [load_half("w1", w1, 0)]
         for q in range(4):
             nc.sync.dma_start(scale_table[32 * q : 32 * q + 4, :].bitcast(I32), x_scales[0, 4 * q : 4 * q + 4, :].bitcast(I32))
+        w1_raw.append(load_half("w1", w1, 1))
+        word_table = keep.tile([P, T], U32, name="word_table")
+        nc.sync.dma_start(word_table[:].bitcast(I32), x_words[0].rearrange("p n t -> p (n t)").bitcast(I32))
         ga_t = load_gain("ga_t", ga, nc.gpsimd)
-        l2, l4 = (load_list(f"l_{k}", n) for k, n in ((2, n2), (4, n4)))
-        w2_raw = load_weight("w2", w2)
+        l1, l3, l2, l4 = (load_list(f"l{k}", n) for k, n in ((1, n1), (3, n3), (2, n2), (4, n4)))
+        w2_raw = [load_half("w2", w2, h) for h in range(2)]
         gb_t = load_gain("gb_t", gb, nc.sync)
         l7, l5, l6, l9, l8, l10 = (load_list(f"l{k}", n) for k, n in ((7, n7), (5, n5), (6, n6), (9, n9), (8, n8), (10, n10)))
 
@@ -102,54 +110,61 @@ def tile_picked_kqdetwsumtop2_none_p_kernel(
             picked.append((codes, scales))
         xa, xb = picked
         nc.vector.tensor_copy(xa[1][:], scale_table[:].indirect(l_offs[:]))
+        nc.vector.tensor_copy(xb[1][:], scale_table[:].indirect(l_two[:]))
         w1q = quantize("w1", cast_weight("w1", w1_raw)[:], N)
         nc.vector.tensor_copy(xa[0][:], word_table[:].indirect(l_offs[:]))
-        nc.vector.tensor_copy(xb[1][:], scale_table[:].indirect(l_two[:]))
         nc.vector.tensor_copy(xb[0][:], word_table[:].indirect(l_two[:]))
 
         banks = [psum.tile([P, N], F32, name=f"bank{u}") for u in range(8)]
         for t in range(4):
             product(banks[t][:], w1q, slice(P * t, P * (t + 1)), xa)
             nc.scalar.activation(gained_win[t][:, :N], banks[t][:], ACT.Copy, scale=ga_t[:, 2 * t : 2 * t + 1])
-            nc.scalar.activation(plain_win[t][:, :N], banks[t][:], ACT.Copy, scale=0.75)
+            nc.scalar.copy(plain_win[t][:, :N], banks[t][:])
+            if t == 1:
+                w2_bf = cast_weight("w2", w2_raw)
 
-        w2q = quantize("w2", cast_weight("w2", w2_raw)[:], N)
-        sig_own = keep.tile([P, PACK, N], F32, name="sig_own")
-        sig_other = keep.tile([P, PACK, N], F32, name="sig_other")
+        w2q = quantize("w2", w2_bf[:], N)
+        spare = keep.tile([P, 3, N], F32, name="spare")
+        sig_own = [raw_b[:, N:]] + [b_win[t][:, N:] for t in range(3)]
+        sig_other = [b_win[3][:, N:]] + [spare[:, t, :] for t in range(3)]
         for t in range(4):
             product(banks[4 + t][:], w2q, slice(P * t, P * (t + 1)), xb)
-            nc.scalar.activation(sig_own[:, t, :], banks[4 + t][:], ACT.Sigmoid)
+            nc.scalar.activation(sig_own[t], banks[4 + t][:], ACT.Sigmoid)
             nc.scalar.copy(raw_b[:, :N], banks[4 + t][:])
-            nc.scalar.activation(sig_other[:, t, :], raw_b[:].indirect(l7[:]), ACT.Sigmoid)
+            nc.scalar.activation(sig_other[t], raw_b[:].indirect(l7[:]), ACT.Sigmoid)
+            nc.scalar.activation(b_win[t][:, :N], banks[4 + t][:], ACT.Copy, scale=gb_t[:, 2 * t : 2 * t + 1])
 
         p12 = keep.tile([P, PACK, N], F32, name="p12")
         p34 = keep.tile([P, PACK, N], F32, name="p34")
         for t in range(4):
-            a1 = work.tile([P, N], F32, name="a1")
+            if t == 2:
+                a1 = keep.tile([P, N], F32, name="a1_late", tag="w2_bf", align_bytes=64)
+            else:
+                a1 = work.tile([P, N], F32, name="a1")
             a3 = work.tile([P, N], F32, name="a3")
-            nc.vector.tensor_copy(a1[:], gained_win[t][:].indirect(l1[:]))
-            nc.vector.tensor_copy(a3[:], gained_win[t][:].indirect(l3[:]))
+            nc.vector.tensor_scalar(a1[:], gained_win[t][:].indirect(l1[:]), 0.75, 0.0, ALU.mult, ALU.add)
+            nc.vector.tensor_scalar(a3[:], gained_win[t][:].indirect(l3[:]), -0.75, 0.0, ALU.mult, ALU.add)
             nc.vector.tensor_tensor(p12[:, t, :], plain_win[t][:].indirect(l2[:]), a1[:], ALU.mult)
             nc.vector.tensor_tensor(p34[:, t, :], plain_win[t][:].indirect(l4[:]), a3[:], ALU.mult)
-            nc.scalar.activation(plain_win[t][:, :N], banks[4 + t][:], ACT.Copy, scale=gb_t[:, 2 * t : 2 * t + 1])
+            for block in range(4):
+                cols = slice(P * block, P * (block + 1))
+                turn(banks[4 + block], t, [p12[:, t, cols], p34[:, t, cols]])
 
-        def make_z(t):
-            z_bf = keep.tile([P, P * PACK], BF16, name=f"z_bf{t}", align_bytes=64)
-            nc.vector.tensor_tensor(
-                z_bf[:].rearrange("p (a i k) -> p a k i", i=2, k=PACK),
-                p12[:].rearrange("p k (a t i) -> p t a k i", t=4, i=2)[:, t],
-                p34[:].rearrange("p k (a t i) -> p t a k i", t=4, i=2)[:, t],
-                ALU.subtract,
-            )
-            return z_bf
+        z_bf = keep.tile([P, N * PACK], BF16, name="z_bf", align_bytes=64)
+        z_words = z_bf[:].bitcast(F32).rearrange("p (t b m u) -> p t b m u", t=4, b=4, u=2)
+        for block in range(4):
+            zt_bf = keep.tile([P, N], BF16, name=f"zt_bf{block}")
+            nc.scalar.copy(zt_bf[:].rearrange("p (u m e) -> p u m e", u=2, e=2), banks[4 + block][:].rearrange("p (u e m) -> p u m e", u=2, e=2))
+            for u in range(2):
+                turn(banks[block // 2], 2 * (block % 2) + u, [zt_bf[:].bitcast(F32)[:, P * u : P * (u + 1)]])
+            if block % 2:
+                nc.scalar.copy(z_words[:, :, block - 1 : block + 1], banks[block // 2][:].rearrange("p (b u m t) -> p t b m u", b=2, u=2, t=4))
 
         p5 = keep.tile([P, PACK, N], F32, name="p5")
         p6 = keep.tile([P, PACK, N], F32, name="p6")
-        z_bf = [make_z(0)]
         for t in range(4):
-            nc.vector.tensor_tensor(p5[:, t, :], plain_win[t][:].indirect(l5[:]), sig_own[:, t, :], ALU.mult)
-            nc.vector.tensor_tensor(p6[:, t, :], plain_win[t][:].indirect(l6[:]), sig_other[:, t, :], ALU.mult)
-        zq = [quantize("z0", z_bf[0][:], P)]
+            nc.vector.tensor_tensor(p5[:, t, :], b_win[t][:].indirect(l5[:]), sig_own[t], ALU.mult)
+            nc.vector.tensor_tensor(p6[:, t, :], b_win[t][:].indirect(l6[:]), sig_other[t], ALU.mult)
 
         z2_bf = []
         for h in range(2):
@@ -162,35 +177,73 @@ def tile_picked_kqdetwsumtop2_none_p_kernel(
                 ALU.add,
             )
             z2_bf.append(half_bf)
+        zq = quantize("z", z_bf[:], N)
         z2q = [quantize(f"z2_{h}", z2_bf[h][:], HALF) for h in range(2)]
-        z_bf.extend(make_z(t) for t in range(1, 4))
-        zq.extend(quantize(f"z{t}", z_bf[t][:], P) for t in range(1, 4))
 
         for t in range(4):
             for h in range(2):
-                cols = slice(h * HALF, (h + 1) * HALF)
-                product(banks[t][:, cols], zq[t], slice(0, P), z2q[h])
-            nc.scalar.activation(gained_win[t][:, :N], banks[t][:], ACT.Copy, scale=0.03125)
+                product(banks[4 + t][:, h * HALF : (h + 1) * HALF], zq, slice(P * t, P * (t + 1)), z2q[h])
+            nc.scalar.activation(gained_win[t][:, :N], banks[4 + t][:], ACT.Copy, scale=-0.03125)
 
-        out_rows = out.rearrange("(a t i) v -> t i a v", t=4, i=2)
-        for pair in ((0, 1), (2, 3)):
-            names = ("b2", "d12", "gap", "hi", "d3", "y", "bend", "res")
-            v = {(name, t): work.tile([P, N], F32, name=name) for name in names for t in pair}
-            for t in pair:
-                nc.vector.tensor_copy(v["b2", t][:], gained_win[t][:].indirect(l9[:]))
-            for t in pair:
-                nc.vector.tensor_tensor(v["d12", t][:], gained_win[t][:].indirect(l8[:]), v["b2", t][:], ALU.subtract)
-                nc.scalar.activation(v["gap", t][:], v["d12", t][:], ACT.Abs)
-            for t in pair:
-                nc.vector.scalar_tensor_tensor(v["hi", t][:], v["d12", t][:], 0.0, v["b2", t][:], ALU.max, ALU.add)
-            for t in pair:
-                nc.vector.tensor_tensor(v["d3", t][:], gained_win[t][:].indirect(l10[:]), v["hi", t][:], ALU.subtract)
-            for t in pair:
-                nc.vector.scalar_tensor_tensor(v["y", t][:], v["gap", t][:], -1.0, v["d3", t][:], ALU.mult, ALU.max)
-            for t in pair:
-                nc.vector.scalar_tensor_tensor(v["bend", t][:], v["y", t][:], -2.0, v["y", t][:], ALU.mult, ALU.min)
-            for t in pair:
-                for cols in (slice(0, HALF), slice(HALF, N)) if t == 3 else (slice(0, N),):
-                    nc.vector.tensor_tensor(v["res", t][:, cols], v["hi", t][:, cols], v["bend", t][:, cols], ALU.subtract)
-                    for i in range(2):
-                        nc.sync.dma_start(out_rows[t, i][:, cols], v["res", t][i:P:2, cols])
+        out_rows = out.rearrange("(m t) v -> t m v", t=4)
+        blocks = [slice(P * block, P * (block + 1)) for block in range(4)]
+        base = [b_win[t][:, :N] for t in range(4)]
+        up = [plain_win[t][:, :N] for t in range(3)]
+        down = [plain_win[t][:, N:] for t in range(3)]
+        line = [b_win[t][:, N:] for t in range(3)]
+        done = [spare[:, t, :] for t in range(3)]
+        hi = [p6[:, 0, :], p6[:, 1, :], up[0]]
+
+        def fetch_base(t):
+            nc.vector.tensor_copy(base[t], gained_win[t][:].indirect(l9[:]))
+
+        def differences(t):
+            nc.vector.tensor_tensor(p12[:, t, :], gained_win[t][:].indirect(l8[:]), base[t], ALU.subtract)
+            nc.vector.tensor_tensor(p34[:, t, :], gained_win[t][:].indirect(l10[:]), base[t], ALU.subtract)
+            nc.scalar.activation(hi[t], p12[:, t, :], ACT.Relu, scale=-1.0)
+
+        def finish_by_turns(t):
+            y = p5[:, t, :]
+            nc.vector.scalar_tensor_tensor(y, p12[:, t, :], 0.0, p34[:, t, :], ALU.max, ALU.min)
+            lead_bank, line_bank, out_bank = (banks[(t + u) % 3] for u in range(3))
+            for block, cols in enumerate(blocks):
+                turn(lead_bank, block, [hi[t][:, cols], y[:, cols]])
+            for block, cols in enumerate(blocks):
+                turn(line_bank, block, [base[t][:, cols], y[:, cols]])
+            nc.scalar.activation(up[t], lead_bank[:], ACT.Relu, scale=2.0)
+            nc.scalar.activation(down[t], lead_bank[:], ACT.Relu, scale=-1.0)
+            nc.scalar.activation(line[t], line_bank[:], ACT.Copy, scale=-1.0)
+            for block, cols in enumerate(blocks):
+                turn(out_bank, block, [up[t][:, cols], down[t][:, cols], line[t][:, cols]])
+            nc.scalar.copy(done[t], out_bank[:])
+            nc.sync.dma_start(out_rows[t], done[t])
+
+        last = gained_win[3]
+        halves = [(slice(h * HALF, (h + 1) * HALF), slice(16 * h, 16 * (h + 1))) for h in range(2)]
+        b2, d12, d3, gap, y = base[3], p12[:, 3, :], p34[:, 3, :], up[1], p5[:, 3, :]
+        lo, bend, res = p6[:, 2, :], p6[:, 3, :], plain_win[3][:, :N]
+        fetch_base(0)
+        fetch_base(1)
+        differences(0)
+        fetch_base(2)
+        finish_by_turns(0)
+        differences(1)
+        nc.vector.tensor_copy(b2[:, halves[0][0]], last[:].indirect(l9[:, halves[0][1]]))
+        finish_by_turns(1)
+        differences(2)
+        finish_by_turns(2)
+        nc.vector.tensor_copy(b2[:, halves[1][0]], last[:].indirect(l9[:, halves[1][1]]))
+        for cols, entries in halves:
+            nc.vector.tensor_tensor(d12[:, cols], last[:].indirect(l8[:, entries]), b2[:, cols], ALU.subtract)
+            nc.scalar.activation(gap[:, cols], d12[:, cols], ACT.Abs)
+        for cols, entries in halves:
+            nc.vector.scalar_tensor_tensor(lo[:, cols], d12[:, cols], 0.0, b2[:, cols], ALU.min, ALU.add)
+        for cols, entries in halves:
+            nc.vector.tensor_tensor(d3[:, cols], last[:].indirect(l10[:, entries]), lo[:, cols], ALU.subtract)
+        for cols, entries in halves:
+            nc.vector.tensor_tensor(y[:, cols], gap[:, cols], d3[:, cols], ALU.min)
+        for cols, entries in halves:
+            nc.vector.scalar_tensor_tensor(bend[:, cols], y[:, cols], -2.0, y[:, cols], ALU.mult, ALU.max)
+        for cols, entries in halves:
+            nc.vector.tensor_tensor(res[:, cols], bend[:, cols], lo[:, cols], ALU.subtract)
+            nc.sync.dma_start(out_rows[3][:, cols], res[:, cols])

@@ -134,116 +134,120 @@ def tile_picked_kqdetwsumtop2_none_p_kernel(
             nc.scalar.activation(sig_other[t], raw_b[:].indirect(l7[:]), ACT.Sigmoid)
             nc.scalar.activation(b_win[t][:, :N], banks[4 + t][:], ACT.Copy, scale=gb_t[:, 2 * t : 2 * t + 1])
 
-        p12 = keep.tile([P, PACK, N], F32, name="p12")
-        p34 = keep.tile([P, PACK, N], F32, name="p34")
-        for t in range(4):
-            if t == 2:
-                a1 = keep.tile([P, N], F32, name="a1_late", tag="w2_bf", align_bytes=64)
-            else:
-                a1 = work.tile([P, N], F32, name="a1")
-            a3 = work.tile([P, N], F32, name="a3")
-            nc.vector.tensor_scalar(a1[:], gained_win[t][:].indirect(l1[:]), 0.75, 0.0, ALU.mult, ALU.add)
-            nc.vector.tensor_scalar(a3[:], gained_win[t][:].indirect(l3[:]), -0.75, 0.0, ALU.mult, ALU.add)
-            nc.vector.tensor_tensor(p12[:, t, :], plain_win[t][:].indirect(l2[:]), a1[:], ALU.mult)
-            nc.vector.tensor_tensor(p34[:, t, :], plain_win[t][:].indirect(l4[:]), a3[:], ALU.mult)
-            for block in range(4):
-                cols = slice(P * block, P * (block + 1))
-                turn(banks[4 + block], t, [p12[:, t, cols], p34[:, t, cols]])
+        blocks = [slice(P * block, P * (block + 1)) for block in range(4)]
+        p12, p34, p5, p6 = (keep.tile([P, PACK, N], F32, name=name) for name in ("p12", "p34", "p5", "p6"))
 
-        z_bf = keep.tile([P, N * PACK], BF16, name="z_bf", align_bytes=64)
-        z_words = z_bf[:].bitcast(F32).rearrange("p (t b m u) -> p t b m u", t=4, b=4, u=2)
-        for block in range(4):
-            zt_bf = keep.tile([P, N], BF16, name=f"zt_bf{block}")
-            nc.scalar.copy(zt_bf[:].rearrange("p (u m e) -> p u m e", u=2, e=2), banks[4 + block][:].rearrange("p (u e m) -> p u m e", u=2, e=2))
-            for u in range(2):
-                turn(banks[block // 2], 2 * (block % 2) + u, [zt_bf[:].bitcast(F32)[:, P * u : P * (u + 1)]])
-            if block % 2:
-                nc.scalar.copy(z_words[:, :, block - 1 : block + 1], banks[block // 2][:].rearrange("p (b u m t) -> p t b m u", b=2, u=2, t=4))
+        def look_up_a(t, a1, a3):
+            nc.vector.tensor_scalar(a1, gained_win[t][:].indirect(l1[:]), 0.75, 0.0, ALU.mult, ALU.add)
+            nc.vector.tensor_scalar(a3, gained_win[t][:].indirect(l3[:]), 0.75, 0.0, ALU.mult, ALU.add)
+            nc.vector.tensor_tensor(p12[:, t, :], plain_win[t][:].indirect(l2[:]), a1, ALU.mult)
+            nc.vector.tensor_tensor(p34[:, t, :], plain_win[t][:].indirect(l4[:]), a3, ALU.mult)
 
-        p5 = keep.tile([P, PACK, N], F32, name="p5")
-        p6 = keep.tile([P, PACK, N], F32, name="p6")
+        first = keep.tile([P, 2, N], F32, name="first")
+        second = keep.tile([P, 2, N], F32, name="second", tag="w2_bf", align_bytes=64)
+        look_up_a(0, first[:, 0, :], first[:, 1, :])
+        look_up_a(1, second[:, 0, :], second[:, 1, :])
+        look_up_a(2, first[:, 0, :], first[:, 1, :])
         for t in range(4):
             nc.vector.tensor_tensor(p5[:, t, :], b_win[t][:].indirect(l5[:]), sig_own[t], ALU.mult)
             nc.vector.tensor_tensor(p6[:, t, :], b_win[t][:].indirect(l6[:]), sig_other[t], ALU.mult)
+            for block, cols in enumerate(blocks):
+                turn(banks[block], t, [p5[:, t, cols], p6[:, t, cols]])
+        look_up_a(3, sig_own[3], sig_other[3])
 
-        z2_bf = []
-        for h in range(2):
-            half_bf = keep.tile([P, HALF * PACK], BF16, name=f"z2_bf{h}", align_bytes=64)
-            cols = slice(h * HALF, (h + 1) * HALF)
-            nc.vector.tensor_tensor(
-                half_bf[:].rearrange("p (a i k) -> p a k i", i=2, k=PACK),
-                p5[:, :, cols].rearrange("p k (a i) -> p a k i", i=2),
-                p6[:, :, cols].rearrange("p k (a i) -> p a k i", i=2),
-                ALU.add,
-            )
-            z2_bf.append(half_bf)
-        zq = quantize("z", z_bf[:], N)
-        z2q = [quantize(f"z2_{h}", z2_bf[h][:], HALF) for h in range(2)]
+        z2_bf = keep.tile([P, N * PACK], BF16, name="z2_bf", align_bytes=64)
+        z2_words = z2_bf[:].bitcast(F32).rearrange("p (b v u) -> p b v u", b=4, u=2)
+        for block in range(4):
+            turned = keep.tile([P, N], BF16, name=f"turned{block}")
+            nc.scalar.copy(turned[:].rearrange("p (u m e) -> p u m e", u=2, e=2), banks[block][:].rearrange("p (u e m) -> p u m e", u=2, e=2))
+            for u in range(2):
+                turn(banks[4 + block // 2], 2 * (block % 2) + u, [turned[:].bitcast(F32)[:, P * u : P * (u + 1)]])
+            if block % 2:
+                nc.scalar.copy(z2_words[:, block - 1 : block + 1], banks[4 + block // 2][:].rearrange("p (b u v) -> p b v u", b=2, u=2))
 
+        z0_bf = keep.tile([P, N], BF16, name="z0_bf", align_bytes=64)
+        z_bf = [z0_bf[:]] + [z2_bf[:, N * t : N * (t + 1)] for t in range(1, 4)]
         for t in range(4):
-            for h in range(2):
-                product(banks[4 + t][:, h * HALF : (h + 1) * HALF], zq, slice(P * t, P * (t + 1)), z2q[h])
-            nc.scalar.activation(gained_win[t][:, :N], banks[4 + t][:], ACT.Copy, scale=-0.03125)
+            nc.vector.tensor_tensor(
+                z_bf[t].rearrange("p (a i k) -> p a k i", i=2, k=PACK),
+                p12[:].rearrange("p k (a t i) -> p t a k i", t=4, i=2)[:, t],
+                p34[:].rearrange("p k (a t i) -> p t a k i", t=4, i=2)[:, t],
+                ALU.subtract,
+            )
+            if t == 0:
+                z2q = quantize("z2", z2_bf[:], N)
+            zq = quantize(f"z_tile{t}", z_bf[t], P)
+            bank = banks[(6 + t) % 8]
+            product(bank[:], zq, slice(0, P), z2q)
+            nc.scalar.activation(gained_win[t][:, :N], bank[:], ACT.Copy, scale=-0.03125)
 
-        out_rows = out.rearrange("(m t) v -> t m v", t=4)
-        blocks = [slice(P * block, P * (block + 1)) for block in range(4)]
+        out_rows = out.rearrange("(a t i) v -> t i a v", t=4, i=2)
+        halves = [slice(h * HALF, (h + 1) * HALF) for h in range(2)]
+        entries = [slice(16 * h, 16 * (h + 1)) for h in range(2)]
         base = [b_win[t][:, :N] for t in range(4)]
         up = [plain_win[t][:, :N] for t in range(3)]
         down = [plain_win[t][:, N:] for t in range(3)]
         line = [b_win[t][:, N:] for t in range(3)]
-        done = [spare[:, t, :] for t in range(3)]
-        hi = [p6[:, 0, :], p6[:, 1, :], up[0]]
+        done = [p6[:, t, :] for t in range(4)]
+        hi = first[:, 0, :]
+
+        def store(t, cols):
+            for i in range(2):
+                nc.sync.dma_start(out_rows[t, i][:, cols], done[t][i:P:2, cols])
 
         def fetch_base(t):
-            nc.vector.tensor_copy(base[t], gained_win[t][:].indirect(l9[:]))
+            nc.vector.tensor_scalar(base[t], gained_win[t][:].indirect(l9[:]), -1.0, 0.0, ALU.mult, ALU.add)
 
         def differences(t):
-            nc.vector.tensor_tensor(p12[:, t, :], gained_win[t][:].indirect(l8[:]), base[t], ALU.subtract)
-            nc.vector.tensor_tensor(p34[:, t, :], gained_win[t][:].indirect(l10[:]), base[t], ALU.subtract)
-            nc.scalar.activation(hi[t], p12[:, t, :], ACT.Relu, scale=-1.0)
+            nc.vector.tensor_tensor(p12[:, t, :], gained_win[t][:].indirect(l8[:]), base[t], ALU.add)
+            nc.vector.tensor_tensor(p34[:, t, :], gained_win[t][:].indirect(l10[:]), base[t], ALU.add)
+            nc.scalar.activation(hi, p12[:, t, :], ACT.Relu, scale=-1.0)
 
-        def finish_by_turns(t):
+        def finish_by_turns(t, line_bank, lead_banks, out_banks):
             y = p5[:, t, :]
             nc.vector.scalar_tensor_tensor(y, p12[:, t, :], 0.0, p34[:, t, :], ALU.max, ALU.min)
-            lead_bank, line_bank, out_bank = (banks[(t + u) % 3] for u in range(3))
             for block, cols in enumerate(blocks):
-                turn(lead_bank, block, [hi[t][:, cols], y[:, cols]])
-            for block, cols in enumerate(blocks):
-                turn(line_bank, block, [base[t][:, cols], y[:, cols]])
-            nc.scalar.activation(up[t], lead_bank[:], ACT.Relu, scale=2.0)
-            nc.scalar.activation(down[t], lead_bank[:], ACT.Relu, scale=-1.0)
-            nc.scalar.activation(line[t], line_bank[:], ACT.Copy, scale=-1.0)
-            for block, cols in enumerate(blocks):
-                turn(out_bank, block, [up[t][:, cols], down[t][:, cols], line[t][:, cols]])
-            nc.scalar.copy(done[t], out_bank[:])
-            nc.sync.dma_start(out_rows[t], done[t])
+                turn(line_bank, block, [base[t][:, cols], hi[:, cols]])
+            nc.scalar.copy(line[t], line_bank[:])
+            for h, half in enumerate(halves):
+                for block in range(2):
+                    cols = blocks[2 * h + block]
+                    turn(lead_banks[h], block, [hi[:, cols], y[:, cols]])
+                nc.scalar.activation(up[t][:, half], lead_banks[h][:, :HALF], ACT.Relu)
+                nc.scalar.activation(down[t][:, half], lead_banks[h][:, :HALF], ACT.Relu, scale=-2.0)
+            for h, half in enumerate(halves):
+                for block in range(2):
+                    cols = blocks[2 * h + block]
+                    turn(out_banks[h], block, [line[t][:, cols], up[t][:, cols], down[t][:, cols]])
+                nc.scalar.copy(done[t][:, half], out_banks[h][:, :HALF])
+            store(t, slice(0, N))
 
         last = gained_win[3]
-        halves = [(slice(h * HALF, (h + 1) * HALF), slice(16 * h, 16 * (h + 1))) for h in range(2)]
-        b2, d12, d3, gap, y = base[3], p12[:, 3, :], p34[:, 3, :], up[1], p5[:, 3, :]
-        lo, bend, res = p6[:, 2, :], p6[:, 3, :], plain_win[3][:, :N]
+        b2, d12, d3, gap, y = base[3], p12[:, 3, :], p34[:, 3, :], hi, p5[:, 3, :]
+        lo, bend = plain_win[3][:, :N], plain_win[3][:, N:]
+        line_bank, lead_banks, out_banks = banks[2], banks[3:5], banks[5:7]
         fetch_base(0)
         fetch_base(1)
-        differences(0)
-        fetch_base(2)
-        finish_by_turns(0)
-        differences(1)
-        nc.vector.tensor_copy(b2[:, halves[0][0]], last[:].indirect(l9[:, halves[0][1]]))
-        finish_by_turns(1)
-        differences(2)
-        finish_by_turns(2)
-        nc.vector.tensor_copy(b2[:, halves[1][0]], last[:].indirect(l9[:, halves[1][1]]))
-        for cols, entries in halves:
-            nc.vector.tensor_tensor(d12[:, cols], last[:].indirect(l8[:, entries]), b2[:, cols], ALU.subtract)
+        for t in range(3):
+            differences(t)
+            if t == 1:
+                fetch_base(2)
+            if t == 2:
+                nc.vector.tensor_copy(b2[:, halves[0]], last[:].indirect(l9[:, entries[0]]))
+            finish_by_turns(t, line_bank, lead_banks, out_banks)
+            line_bank, lead_banks, out_banks = lead_banks[1], out_banks, [line_bank, lead_banks[0]]
+        nc.vector.tensor_copy(b2[:, halves[1]], last[:].indirect(l9[:, entries[1]]))
+        for cols, part in zip(halves, entries):
+            nc.vector.tensor_tensor(d12[:, cols], last[:].indirect(l8[:, part]), b2[:, cols], ALU.subtract)
             nc.scalar.activation(gap[:, cols], d12[:, cols], ACT.Abs)
-        for cols, entries in halves:
+        for cols in halves:
             nc.vector.scalar_tensor_tensor(lo[:, cols], d12[:, cols], 0.0, b2[:, cols], ALU.min, ALU.add)
-        for cols, entries in halves:
-            nc.vector.tensor_tensor(d3[:, cols], last[:].indirect(l10[:, entries]), lo[:, cols], ALU.subtract)
-        for cols, entries in halves:
+        for cols, part in zip(halves, entries):
+            nc.vector.tensor_tensor(d3[:, cols], last[:].indirect(l10[:, part]), lo[:, cols], ALU.subtract)
+        for cols in halves:
             nc.vector.tensor_tensor(y[:, cols], gap[:, cols], d3[:, cols], ALU.min)
-        for cols, entries in halves:
+        for cols in halves:
             nc.vector.scalar_tensor_tensor(bend[:, cols], y[:, cols], -2.0, y[:, cols], ALU.mult, ALU.max)
-        for cols, entries in halves:
-            nc.vector.tensor_tensor(res[:, cols], bend[:, cols], lo[:, cols], ALU.subtract)
-            nc.sync.dma_start(out_rows[3][:, cols], res[:, cols])
+        for cols in halves:
+            nc.vector.tensor_tensor(done[3][:, cols], bend[:, cols], lo[:, cols], ALU.subtract)
+            store(3, cols)

from contextlib import ExitStack

import concourse.mybir as mybir
from concourse.masks import make_identity

F32 = mybir.dt.float32
BF16 = mybir.dt.bfloat16
I32 = mybir.dt.int32
U32 = mybir.dt.uint32
U16 = mybir.dt.uint16
U8 = mybir.dt.uint8
FP8X4 = mybir.dt.float8_e4m3fn_x4
ALU = mybir.AluOpType
ACT = mybir.ActivationFunctionType

P = 128
PACK = 4
T = 2048
N = 512
WINDOW = 2 * N
HALF = N // 2
FLOPS = 3 * 2 * 512 * 512 * 512


def tile_picked_kqdetwsumtop2_none_p_kernel(
    tc, x_words, x_scales, w1, w2, ga, gb, offs, two, n1, n2, n3, n4, n5, n6, n7, n8, n9, n10, out
):
    nc = tc.nc
    with ExitStack() as ctx:
        keep = ctx.enter_context(tc.tile_pool(name="keep", bufs=1))
        work = ctx.enter_context(tc.tile_pool(name="work", bufs=2))
        psum = ctx.enter_context(tc.psum_pool(name="psum", bufs=1))

        def load_list(name, source):
            tile = keep.tile([P, N // 16], U16, name=name)
            nc.sync.dma_start(tile[:], source)
            return tile

        def load_half(name, w, h):
            raw = keep.tile([P, PACK, HALF], F32, name=f"{name}_raw{h}")
            nc.sync.dma_start(raw[:], w.rearrange("(p j) c -> p j c", j=PACK)[:, :, h * HALF : (h + 1) * HALF])
            return raw

        def load_gain(name, gain, queue):
            tile = keep.tile([P, 8], F32, name=name)
            rows = gain.rearrange("(a e) o -> a (e o)", e=8)
            for i in range(2):
                queue.dma_start(tile[i:P:2, 0:7], rows[:, i : i + 7])
            return tile

        def cast_weight(name, halves):
            grouped = keep.tile([P, N * PACK], BF16, name=f"{name}_bf", align_bytes=64)
            dealt = grouped[:].rearrange("p (t a i j) -> p t a j i", t=4, i=2, j=PACK)
            for h, raw in enumerate(halves):
                nc.scalar.copy(dealt[:, :, 32 * h : 32 * (h + 1)], raw[:].rearrange("p j (a t i) -> p t a j i", t=4, i=2))
            return grouped

        def quantize(name, values, width):
            codes = keep.tile([P, width], U32, name=f"{name}_codes", align_bytes=64)
            scales = keep.tile([P, width], U8, name=f"{name}_scales", align_bytes=64)
            nc.vector.quantize_mx(out=codes[:].bitcast(FP8X4), scales=scales[:], in_=values)
            return codes, scales

        def product(acc, lhs, lhs_cols, rhs):
            nc.tensor.matmul_mx(
                out=acc,
                lhsT=lhs[0][:, lhs_cols].bitcast(FP8X4),
                lhsT_scale=lhs[1][:, lhs_cols],
                rhs=rhs[0][:].bitcast(FP8X4),
                rhs_scale=rhs[1][:],
                start=True,
                stop=True,
            )

        def turn(bank, region, terms):
            for u, term in enumerate(terms):
                nc.tensor.matmul(
                    bank[:, P * region : P * (region + 1)], term, ident[:], is_transpose=True, start=(u == 0), stop=(u == len(terms) - 1)
                )

        scale_table = keep.tile([P, T], U8, name="scale_table")
        nc.vector.memset(scale_table[:].bitcast(I32), 0)
        windows = [keep.tile([P, WINDOW], F32, name=f"window{u}") for u in range(13)]
        gained_win, plain_win, b_win, raw_b = windows[0:4], windows[4:8], windows[8:12], windows[12]
        for window in windows[0:5]:
            nc.vector.memset(window[:, N:].bitcast(I32), 0)
        for window in windows[5:8]:
            nc.scalar.activation(window[:, N:], windows[0][:, N:], ACT.Sigmoid)

        ident = keep.tile([P, P], F32, name="ident")
        make_identity(nc, ident[:])

        l_offs, l_two = load_list("l_offs", offs), load_list("l_two", two)
        w1_raw = [load_half("w1", w1, 0)]
        for q in range(4):
            nc.sync.dma_start(scale_table[32 * q : 32 * q + 4, :].bitcast(I32), x_scales[0, 4 * q : 4 * q + 4, :].bitcast(I32))
        w1_raw.append(load_half("w1", w1, 1))
        word_table = keep.tile([P, T], U32, name="word_table")
        nc.sync.dma_start(word_table[:].bitcast(I32), x_words[0].rearrange("p n t -> p (n t)").bitcast(I32))
        ga_t = load_gain("ga_t", ga, nc.gpsimd)
        l1, l3, l2, l4 = (load_list(f"l{k}", n) for k, n in ((1, n1), (3, n3), (2, n2), (4, n4)))
        w2_raw = [load_half("w2", w2, h) for h in range(2)]
        gb_t = load_gain("gb_t", gb, nc.sync)
        l7, l5, l6, l9, l8, l10 = (load_list(f"l{k}", n) for k, n in ((7, n7), (5, n5), (6, n6), (9, n9), (8, n8), (10, n10)))

        picked = []
        for name in ("xa", "xb"):
            codes = keep.tile([P, N], U32, name=f"{name}_codes", align_bytes=64)
            scales = keep.tile([P, N], U8, name=f"{name}_scales", align_bytes=64)
            picked.append((codes, scales))
        xa, xb = picked
        nc.vector.tensor_copy(xa[1][:], scale_table[:].indirect(l_offs[:]))
        nc.vector.tensor_copy(xb[1][:], scale_table[:].indirect(l_two[:]))
        w1q = quantize("w1", cast_weight("w1", w1_raw)[:], N)
        nc.vector.tensor_copy(xa[0][:], word_table[:].indirect(l_offs[:]))
        nc.vector.tensor_copy(xb[0][:], word_table[:].indirect(l_two[:]))

        banks = [psum.tile([P, N], F32, name=f"bank{u}") for u in range(8)]
        for t in range(4):
            product(banks[t][:], w1q, slice(P * t, P * (t + 1)), xa)
            nc.scalar.activation(gained_win[t][:, :N], banks[t][:], ACT.Copy, scale=ga_t[:, 2 * t : 2 * t + 1])
            nc.scalar.copy(plain_win[t][:, :N], banks[t][:])
            if t == 1:
                w2_bf = cast_weight("w2", w2_raw)

        w2q = quantize("w2", w2_bf[:], N)
        spare = keep.tile([P, 3, N], F32, name="spare")
        sig_own = [raw_b[:, N:]] + [b_win[t][:, N:] for t in range(3)]
        sig_other = [b_win[3][:, N:]] + [spare[:, t, :] for t in range(3)]
        for t in range(4):
            product(banks[4 + t][:], w2q, slice(P * t, P * (t + 1)), xb)
            nc.scalar.activation(sig_own[t], banks[4 + t][:], ACT.Sigmoid)
            nc.scalar.copy(raw_b[:, :N], banks[4 + t][:])
            nc.scalar.activation(sig_other[t], raw_b[:].indirect(l7[:]), ACT.Sigmoid)
            nc.scalar.activation(b_win[t][:, :N], banks[4 + t][:], ACT.Copy, scale=gb_t[:, 2 * t : 2 * t + 1])

        blocks = [slice(P * block, P * (block + 1)) for block in range(4)]
        p12, p34, p5, p6 = (keep.tile([P, PACK, N], F32, name=name) for name in ("p12", "p34", "p5", "p6"))

        def look_up_a(t, a1, a3):
            nc.vector.tensor_scalar(a1, gained_win[t][:].indirect(l1[:]), 0.75, 0.0, ALU.mult, ALU.add)
            nc.vector.tensor_scalar(a3, gained_win[t][:].indirect(l3[:]), 0.75, 0.0, ALU.mult, ALU.add)
            nc.vector.tensor_tensor(p12[:, t, :], plain_win[t][:].indirect(l2[:]), a1, ALU.mult)
            nc.vector.tensor_tensor(p34[:, t, :], plain_win[t][:].indirect(l4[:]), a3, ALU.mult)

        first = keep.tile([P, 2, N], F32, name="first")
        second = keep.tile([P, 2, N], F32, name="second", tag="w2_bf", align_bytes=64)
        look_up_a(0, first[:, 0, :], first[:, 1, :])
        look_up_a(1, second[:, 0, :], second[:, 1, :])
        look_up_a(2, first[:, 0, :], first[:, 1, :])
        for t in range(4):
            nc.vector.tensor_tensor(p5[:, t, :], b_win[t][:].indirect(l5[:]), sig_own[t], ALU.mult)
            nc.vector.tensor_tensor(p6[:, t, :], b_win[t][:].indirect(l6[:]), sig_other[t], ALU.mult)
            for block, cols in enumerate(blocks):
                turn(banks[block], t, [p5[:, t, cols], p6[:, t, cols]])
        look_up_a(3, sig_own[3], sig_other[3])

        z2_bf = keep.tile([P, N * PACK], BF16, name="z2_bf", align_bytes=64)
        z2_words = z2_bf[:].bitcast(F32).rearrange("p (b v u) -> p b v u", b=4, u=2)
        for block in range(4):
            turned = keep.tile([P, N], BF16, name=f"turned{block}")
            nc.scalar.copy(turned[:].rearrange("p (u m e) -> p u m e", u=2, e=2), banks[block][:].rearrange("p (u e m) -> p u m e", u=2, e=2))
            for u in range(2):
                turn(banks[4 + block // 2], 2 * (block % 2) + u, [turned[:].bitcast(F32)[:, P * u : P * (u + 1)]])
            if block % 2:
                nc.scalar.copy(z2_words[:, block - 1 : block + 1], banks[4 + block // 2][:].rearrange("p (b u v) -> p b v u", b=2, u=2))

        z0_bf = keep.tile([P, N], BF16, name="z0_bf", align_bytes=64)
        z_bf = [z0_bf[:]] + [z2_bf[:, N * t : N * (t + 1)] for t in range(1, 4)]
        for t in range(4):
            nc.vector.tensor_tensor(
                z_bf[t].rearrange("p (a i k) -> p a k i", i=2, k=PACK),
                p12[:].rearrange("p k (a t i) -> p t a k i", t=4, i=2)[:, t],
                p34[:].rearrange("p k (a t i) -> p t a k i", t=4, i=2)[:, t],
                ALU.subtract,
            )
            if t == 0:
                z2q = quantize("z2", z2_bf[:], N)
            zq = quantize(f"z_tile{t}", z_bf[t], P)
            bank = banks[(6 + t) % 8]
            product(bank[:], zq, slice(0, P), z2q)
            nc.scalar.activation(gained_win[t][:, :N], bank[:], ACT.Copy, scale=-0.03125)

        out_rows = out.rearrange("(a t i) v -> t i a v", t=4, i=2)
        halves = [slice(h * HALF, (h + 1) * HALF) for h in range(2)]
        entries = [slice(16 * h, 16 * (h + 1)) for h in range(2)]
        base = [b_win[t][:, :N] for t in range(4)]
        up = [plain_win[t][:, :N] for t in range(3)]
        down = [plain_win[t][:, N:] for t in range(3)]
        line = [b_win[t][:, N:] for t in range(3)]
        done = [p6[:, t, :] for t in range(4)]
        hi = first[:, 0, :]

        def store(t, cols):
            for i in range(2):
                nc.sync.dma_start(out_rows[t, i][:, cols], done[t][i:P:2, cols])

        def fetch_base(t):
            nc.vector.tensor_scalar(base[t], gained_win[t][:].indirect(l9[:]), -1.0, 0.0, ALU.mult, ALU.add)

        def differences(t):
            nc.vector.tensor_tensor(p12[:, t, :], gained_win[t][:].indirect(l8[:]), base[t], ALU.add)
            nc.vector.tensor_tensor(p34[:, t, :], gained_win[t][:].indirect(l10[:]), base[t], ALU.add)
            nc.scalar.activation(hi, p12[:, t, :], ACT.Relu, scale=-1.0)

        def finish_by_turns(t, line_bank, lead_banks, out_banks):
            y = p5[:, t, :]
            nc.vector.scalar_tensor_tensor(y, p12[:, t, :], 0.0, p34[:, t, :], ALU.max, ALU.min)
            for block, cols in enumerate(blocks):
                turn(line_bank, block, [base[t][:, cols], hi[:, cols]])
            nc.scalar.copy(line[t], line_bank[:])
            for h, half in enumerate(halves):
                for block in range(2):
                    cols = blocks[2 * h + block]
                    turn(lead_banks[h], block, [hi[:, cols], y[:, cols]])
                nc.scalar.activation(up[t][:, half], lead_banks[h][:, :HALF], ACT.Relu)
                nc.scalar.activation(down[t][:, half], lead_banks[h][:, :HALF], ACT.Relu, scale=-2.0)
            for h, half in enumerate(halves):
                for block in range(2):
                    cols = blocks[2 * h + block]
                    turn(out_banks[h], block, [line[t][:, cols], up[t][:, cols], down[t][:, cols]])
                nc.scalar.copy(done[t][:, half], out_banks[h][:, :HALF])
            store(t, slice(0, N))

        last = gained_win[3]
        b2, d12, d3, gap, y = base[3], p12[:, 3, :], p34[:, 3, :], hi, p5[:, 3, :]
        lo, bend = plain_win[3][:, :N], plain_win[3][:, N:]
        line_bank, lead_banks, out_banks = banks[2], banks[3:5], banks[5:7]
        fetch_base(0)
        fetch_base(1)
        for t in range(3):
            differences(t)
            if t == 1:
                fetch_base(2)
            if t == 2:
                nc.vector.tensor_copy(b2[:, halves[0]], last[:].indirect(l9[:, entries[0]]))
            finish_by_turns(t, line_bank, lead_banks, out_banks)
            line_bank, lead_banks, out_banks = lead_banks[1], out_banks, [line_bank, lead_banks[0]]
        nc.vector.tensor_copy(b2[:, halves[1]], last[:].indirect(l9[:, entries[1]]))
        for cols, part in zip(halves, entries):
            nc.vector.tensor_tensor(d12[:, cols], last[:].indirect(l8[:, part]), b2[:, cols], ALU.subtract)
            nc.scalar.activation(gap[:, cols], d12[:, cols], ACT.Abs)
        for cols in halves:
            nc.vector.scalar_tensor_tensor(lo[:, cols], d12[:, cols], 0.0, b2[:, cols], ALU.min, ALU.add)
        for cols, part in zip(halves, entries):
            nc.vector.tensor_tensor(d3[:, cols], last[:].indirect(l10[:, part]), lo[:, cols], ALU.subtract)
        for cols in halves:
            nc.vector.tensor_tensor(y[:, cols], gap[:, cols], d3[:, cols], ALU.min)
        for cols in halves:
            nc.vector.scalar_tensor_tensor(bend[:, cols], y[:, cols], -2.0, y[:, cols], ALU.mult, ALU.max)
        for cols in halves:
            nc.vector.tensor_tensor(done[3][:, cols], bend[:, cols], lo[:, cols], ALU.subtract)
            store(3, cols)
